import numpy as np
import ml_dtypes


def mxq(x, axis, fmt="e4m3"):
    dtype, down = {"e4m3": (ml_dtypes.float8_e4m3fn, 7), "e5m2": (ml_dtypes.float8_e5m2, 14)}[fmt]
    v = np.moveaxis(np.asarray(x, np.float32).astype(ml_dtypes.bfloat16).astype(np.float64), axis, -1)
    blocks = v.reshape(v.shape[:-1] + (-1, 32))
    amax = np.abs(blocks).max(-1, keepdims=True)
    byte = np.maximum(np.where(amax > 0, np.frexp(amax)[1] - 1 + 127, 0) - down, 1)
    scale = np.exp2(byte - 127.0)
    codes = (blocks / scale).astype(np.float32).astype(dtype).astype(np.float64)
    return np.moveaxis((codes * scale).reshape(v.shape), -1, axis)


WIDE = False


def mx_kscale(k):
    if not WIDE:
        return np.ones(k)
    levels = np.array([30, -30])
    if k % 512:
        return np.exp2(np.random.permutation(np.resize(levels, k // 32))).repeat(32)
    a = np.empty((k // 512, 16))
    for p in range(k // 512):
        a[p, :8] = np.random.permutation(np.resize(levels, 8))
        for g in range(8):
            far = levels[np.abs(levels - a[p, g]) >= 10]
            a[p, g + 8] = far[np.random.randint(len(far))]
    return np.exp2(a.ravel()).repeat(32)


def f64(x):
    return np.asarray(x).astype(np.float64)


def striped(idx):
    return np.tile(np.asarray(idx).reshape(-1, 16).T, (8, 1)).astype(np.uint16)


def unstriped(offs):
    return offs[:16].T.reshape(-1).astype(np.int64)


E2M1 = np.array([0.0, 0.5, 1.0, 1.5, 2.0, 3.0, 4.0, 6.0, -0.0, -0.5, -1.0, -1.5, -2.0, -3.0, -4.0, -6.0])


def pack_weight(w, fmt):
    k, n = w.shape
    w = f64(np.asarray(w, np.float32).astype(ml_dtypes.bfloat16)).reshape(k // 32, 32, n)
    amax = np.abs(w).max(1)
    if fmt in ("e4m3", "e5m2"):
        byte = np.frexp(amax)[1] - 1 + 127 - (7 if fmt == "e4m3" else 14)
    else:
        mant, ex = np.frexp(amax / 6.0)
        byte = np.where(mant > 0.5, ex, ex - 1) + 127
    byte = np.clip(np.where(amax > 0, byte, 1), 1, 254)
    scaled = (w * np.exp2(127.0 - byte)[:, None, :]).reshape(k, n).astype(np.float32)
    by_word = np.ascontiguousarray(scaled.reshape(k // 512, 128, 4, n).transpose(0, 1, 3, 2))
    if fmt in ("e4m3", "e5m2"):
        words = by_word.astype(ml_dtypes.float8_e4m3fn if fmt == "e4m3" else ml_dtypes.float8_e5m2).view(np.uint8)
    else:
        c = by_word.astype(ml_dtypes.float4_e2m1fn).view(np.uint8) & 0xF
        words = (c[..., 0::2] | (c[..., 1::2] << 4)).reshape(k // 512, 128, 2 * n)
    return np.ascontiguousarray(words), np.ascontiguousarray(byte.astype(np.uint8).reshape(k // 512, 16, n))


def unpack_weight(words, scales, fmt):
    g, _, n = scales.shape
    words = np.ascontiguousarray(words).reshape(g, 128, n, -1)
    if fmt in ("e4m3", "e5m2"):
        vals = words.view(ml_dtypes.float8_e4m3fn if fmt == "e4m3" else ml_dtypes.float8_e5m2).astype(np.float64)
    else:
        nib = np.empty((g, 128, n, 4), np.uint8)
        nib[..., 0::2] = words & 0xF
        nib[..., 1::2] = words >> 4
        vals = E2M1[nib]
    vals = vals * np.repeat(np.exp2(scales.astype(np.float64) - 127.0), 8, axis=1)[..., None]
    return vals.transpose(0, 1, 3, 2).reshape(g * 512, n)


K, F, T, Z, J, R, N = 512, 512, 1024, 1024, 256, 512, 256


def setup_inputs():
    n = np.random.standard_normal
    idx = np.random.permutation(T)[:J]
    idx2 = np.random.permutation(Z)[:J]
    idx3 = np.random.permutation(J)[:J]
    idx4 = np.random.permutation(T)[:J]
    fk = mx_kscale(K)
    fr = mx_kscale(R)
    ff = mx_kscale(F)
    xtp = pack_weight(n((K, T)) / fk[:, None], "e4m3")
    wp = pack_weight(n((K, R)) * 1 / np.sqrt(K) * fk[:, None] * fr, "e2m1")
    xop = pack_weight(n((F, Z)) / ff[:, None], "e2m1")
    w2p = pack_weight(n((F, R)) * 1 / np.sqrt(F) * ff[:, None] * fr, "e5m2")
    wbp = pack_weight(n((R, N)) * 1 / np.sqrt(R) / fr[:, None], "e5m2")
    wsp = pack_weight(n((K, N)) * 1 / np.sqrt(K) * fk[:, None], "e5m2")
    return {
        "xt_words": xtp[0],
        "xt_scales": xtp[1],
        "w_words": wp[0],
        "w_scales": wp[1],
        "xo_words": xop[0],
        "xo_scales": xop[1],
        "w2_words": w2p[0],
        "w2_scales": w2p[1],
        "wb_words": wbp[0],
        "wb_scales": wbp[1],
        "ws_words": wsp[0],
        "ws_scales": wsp[1],
        "offs": striped(idx),
        "offs2": striped(idx2),
        "offs3": striped(idx3),
        "offs4": striped(idx4),
    }


def reference(xt_words, xt_scales, w_words, w_scales, xo_words, xo_scales, w2_words, w2_scales, wb_words, wb_scales, ws_words, ws_scales, offs, offs2, offs3, offs4):
    idx = unstriped(offs)
    idx2 = unstriped(offs2)
    idx3 = unstriped(offs3)
    idx4 = unstriped(offs4)
    xtu = unpack_weight(xt_words, xt_scales, "e4m3")
    wu = unpack_weight(w_words, w_scales, "e2m1")
    xou = unpack_weight(xo_words, xo_scales, "e2m1")
    w2u = unpack_weight(w2_words, w2_scales, "e5m2")
    wbu = unpack_weight(wb_words, wb_scales, "e5m2")
    wsu = unpack_weight(ws_words, ws_scales, "e5m2")
    xtidxg = xtu[:, idx]
    a = wu.T @ xtidxg
    xoidx2g = xou[:, idx2]
    b = w2u.T @ xoidx2g
    hid = np.maximum(a, b[:, idx3])
    hidq = mxq(hid, 0, "e4m3")
    xtidx4g = xtu[:, idx4]
    y = wbu.T @ hidq + wsu.T @ xtidx4g
    return y

@@ -1,0 +1,165 @@
+from contextlib import ExitStack
+
+import concourse.mybir as mybir
+
+K, F, T, Z, J, R, N = 512, 512, 1024, 1024, 256, 512, 256
+FLOPS = 2 * J * (K * R + F * R + R * N + K * N)
+
+F32 = mybir.dt.float32
+BF16 = mybir.dt.bfloat16
+I32 = mybir.dt.int32
+U32 = mybir.dt.uint32
+U16 = mybir.dt.uint16
+U8 = mybir.dt.uint8
+E4M3 = mybir.dt.float8_e4m3fn_x4
+E5M2 = mybir.dt.float8_e5m2_x4
+E2M1 = mybir.dt.float4_e2m1fn_x4
+COPY = mybir.ActivationFunctionType.Copy
+MAX = mybir.AluOpType.max
+
+P = 128
+PACK = 4
+HALF = J // 2
+
+
+def load_scales(low_queue, high_queue, plane, scales):
+    rows = scales[0].bitcast(I32)
+    words = plane.bitcast(I32)
+    low_queue.dma_start(out=words[0:84, :], in_=rows[0:14, :].partition_broadcast(6))
+    high_queue.dma_start(out=words[84:128, :], in_=rows[12:16, :].partition_broadcast(11))
+
+
+def tile_list_partner_twotab_further_plain_kernel(
+    tc, xt_words, xt_scales, w_words, w_scales, xo_words, xo_scales, w2_words, w2_scales,
+    wb_words, wb_scales, ws_words, ws_scales, offs, offs2, offs3, offs4, out,
+):
+    nc = tc.nc
+    with ExitStack() as ctx:
+        sb = ctx.enter_context(tc.tile_pool(name="sb", bufs=1))
+        ps = ctx.enter_context(tc.psum_pool(name="ps", bufs=1))
+
+        def tile(name, cols, dtype):
+            return sb.tile([P, cols], dtype, name=name, align_bytes=64)
+
+        list1 = tile("list1", J // 16, U16)
+        list2 = tile("list2", J // 16, U16)
+        list3 = tile("list3", J // 16, U16)
+        list4 = tile("list4", J // 16, U16)
+        xt_w = tile("xt_w", T, U32)
+        xt_s = tile("xt_s", T, U8)
+        xo_w = tile("xo_w", Z, U16)
+        xo_s = tile("xo_s", Z, U8)
+        w_w = tile("w_w", R, U16)
+        w_s = tile("w_s", R, U8)
+        w2_w = tile("w2_w", R, U32)
+        w2_s = tile("w2_s", R, U8)
+        wb_w = tile("wb_w", N, U32)
+        wb_s = tile("wb_s", N, U8)
+        ws_w = tile("ws_w", N, U32)
+        ws_s = tile("ws_s", N, U8)
+
+        def words4(ap):
+            return ap[0].rearrange("p c t -> p (c t)").bitcast(I32)
+
+        nc.sync.dma_start(out=xo_w[:].bitcast(I32), in_=xo_words[0].bitcast(I32))
+        nc.sync.dma_start(list2[:], offs2)
+        load_scales(nc.scalar, nc.sync, xo_s[:], xo_scales)
+        nc.sync.dma_start(out=w2_w[:].bitcast(I32), in_=words4(w2_words))
+        load_scales(nc.scalar, nc.sync, w2_s[:], w2_scales)
+        nc.sync.dma_start(out=xt_w[:].bitcast(I32), in_=words4(xt_words))
+        nc.sync.dma_start(list1[:], offs)
+        load_scales(nc.scalar, nc.sync, xt_s[:], xt_scales)
+        nc.sync.dma_start(out=w_w[:].bitcast(I32), in_=w_words[0].bitcast(I32))
+        load_scales(nc.sync, nc.sync, w_s[:], w_scales)
+        nc.sync.dma_start(list3[:], offs3)
+        nc.sync.dma_start(list4[:], offs4)
+        nc.sync.dma_start(out=ws_w[:].bitcast(I32), in_=words4(ws_words))
+        nc.sync.dma_start(out=wb_w[:].bitcast(I32), in_=words4(wb_words))
+        load_scales(nc.gpsimd, nc.gpsimd, ws_s[:], ws_scales)
+        load_scales(nc.gpsimd, nc.gpsimd, wb_s[:], wb_scales)
+
+        def gather(name, table, offsets, dtype):
+            picked = tile(name, J, dtype)
+            nc.vector.tensor_copy(picked[:], table[:].indirect(offsets[:]))
+            return picked
+
+        def deal(copy, name, src, dtype):
+            dealt = tile(name, R, dtype)
+            copy(dealt[:].rearrange("p (t m) -> p t m", t=PACK), src[:].rearrange("p (m t) -> p t m", t=PACK))
+            return dealt
+
+        xo_gw = gather("xo_gw", xo_w, list2, U16)
+        xo_gs = gather("xo_gs", xo_s, list2, U8)
+        w2_dw = deal(nc.scalar.copy, "w2_dw", w2_w, U32)
+        w2_ds = deal(nc.vector.tensor_copy, "w2_ds", w2_s, U8)
+        w_dw = deal(nc.scalar.copy, "w_dw", w_w, U16)
+        xt_gw = gather("xt_gw", xt_w, list1, U32)
+        xt_gs = gather("xt_gs", xt_s, list1, U8)
+        w_ds = deal(nc.vector.tensor_copy, "w_ds", w_s, U8)
+
+        b_sb = []
+        for t in range(PACK):
+            cols = slice(t * P, (t + 1) * P)
+            b_ps = ps.tile([P, J], F32, name="b_ps%d" % t)
+            nc.tensor.matmul_mx(
+                out=b_ps[:], lhsT=w2_dw[:, cols].bitcast(E5M2), lhsT_scale=w2_ds[:, cols],
+                rhs=xo_gw[:].bitcast(E2M1), rhs_scale=xo_gs[:], start=True, stop=True,
+            )
+            b_t = tile("b%d" % t, J, F32)
+            nc.scalar.activation(out=b_t[:], in_=b_ps[:], func=COPY)
+            b_sb.append(b_t)
+
+        halves = [slice(h * HALF, (h + 1) * HALF) for h in range(2)]
+        a_ps = [ps.tile([P, PACK, HALF], F32, name="a_ps%d" % h) for h in range(2)]
+        y_ps = [ps.tile([P, N // P, HALF], F32, name="y_ps%d" % h) for h in range(2)]
+        partner = [sb.tile([P, PACK, HALF], F32, name="partner%d" % h, align_bytes=64) for h in range(2)]
+        hid = [sb.tile([P, HALF, PACK], BF16, name="hid%d" % h, align_bytes=64) for h in range(2)]
+        for h in range(2):
+            for t in range(PACK):
+                cols = slice(t * P, (t + 1) * P)
+                nc.tensor.matmul_mx(
+                    out=a_ps[h][:, t, :], lhsT=w_dw[:, cols].bitcast(E2M1), lhsT_scale=w_ds[:, cols],
+                    rhs=xt_gw[:, halves[h]].bitcast(E4M3), rhs_scale=xt_gs[:, halves[h]], start=True, stop=True,
+                )
+
+        for h in range(2):
+            for t in range(PACK):
+                picked = b_sb[t][:].indirect(list3[:, h * HALF // 16 : (h + 1) * HALF // 16])
+                if h == 0 and t < 2:
+                    nc.vector.tensor_copy(partner[h][:, t, :], picked)
+                else:
+                    nc.scalar.activation(out=partner[h][:, t, :], in_=picked, func=COPY)
+
+        def larger(h):
+            nc.vector.tensor_tensor(
+                out=hid[h][:], in0=a_ps[h][:].rearrange("p t j -> p j t"),
+                in1=partner[h][:].rearrange("p t j -> p j t"), op=MAX,
+            )
+
+        def finish(h):
+            hid_w = tile("hid_w%d" % h, HALF, U32)
+            hid_s = tile("hid_s%d" % h, HALF, U8)
+            nc.vector.quantize_mx(out=hid_w[:].bitcast(E4M3), scales=hid_s[:], in_=hid[h][:].rearrange("p j t -> p (j t)"))
+            for m in range(N // P):
+                cols = slice(m * P, (m + 1) * P)
+                nc.tensor.matmul_mx(
+                    out=y_ps[h][:, m, :], lhsT=wb_w[:, cols].bitcast(E5M2), lhsT_scale=wb_s[:, cols],
+                    rhs=hid_w[:].bitcast(E4M3), rhs_scale=hid_s[:], start=False, stop=(m == N // P - 1),
+                )
+            y = sb.tile([P, N // P, HALF], F32, name="y%d" % h, align_bytes=64)
+            nc.scalar.copy(y[:], y_ps[h][:])
+            nc.sync.dma_start(out=out.rearrange("(m p) j -> p m j", p=P)[:, :, halves[h]], in_=y[:])
+
+        xs_gw = gather("xs_gw", xt_w, list4, U32)
+        larger(0)
+        xs_gs = gather("xs_gs", xt_s, list4, U8)
+        for h in range(2):
+            for m in range(N // P):
+                cols = slice(m * P, (m + 1) * P)
+                nc.tensor.matmul_mx(
+                    out=y_ps[h][:, m, :], lhsT=ws_w[:, cols].bitcast(E5M2), lhsT_scale=ws_s[:, cols],
+                    rhs=xs_gw[:, halves[h]].bitcast(E4M3), rhs_scale=xs_gs[:, halves[h]], start=(m == 0), stop=False,
+                )
+        finish(0)
+        larger(1)
+        finish(1)

@@ -22,11 +22,12 @@ PACK = 4
 HALF = J // 2
 
 
-def load_scales(low_queue, high_queue, plane, scales):
-    rows = scales[0].bitcast(I32)
-    words = plane.bitcast(I32)
-    low_queue.dma_start(out=words[0:84, :], in_=rows[0:14, :].partition_broadcast(6))
-    high_queue.dma_start(out=words[84:128, :], in_=rows[12:16, :].partition_broadcast(11))
+def load_low(queue, plane, scales):
+    queue.dma_start(out=plane[0:16, :].bitcast(I32), in_=scales[0].bitcast(I32))
+
+
+def load_high(queue, plane, scales):
+    queue.dma_start(out=plane[16:128, :].bitcast(I32), in_=scales[0, 2:16, :].bitcast(I32).partition_broadcast(8))
 
 
 def tile_list_partner_twotab_further_plain_kernel(
@@ -50,57 +51,65 @@ def tile_list_partner_twotab_further_plain_kernel(
         xo_w = tile("xo_w", Z, U16)
         xo_s = tile("xo_s", Z, U8)
         w_w = tile("w_w", R, U16)
-        w_s = tile("w_s", R, U8)
         w2_w = tile("w2_w", R, U32)
-        w2_s = tile("w2_s", R, U8)
         wb_w = tile("wb_w", N, U32)
-        wb_s = tile("wb_s", N, U8)
         ws_w = tile("ws_w", N, U32)
+        w2_s = tile("w2_s", R, U8)
+        w_s = tile("w_s", R, U8)
         ws_s = tile("ws_s", N, U8)
+        wb_s = tile("wb_s", N, U8)
 
         def words4(ap):
             return ap[0].rearrange("p c t -> p (c t)").bitcast(I32)
 
         nc.sync.dma_start(out=xo_w[:].bitcast(I32), in_=xo_words[0].bitcast(I32))
+        load_high(nc.scalar, xo_s, xo_scales)
+        load_high(nc.gpsimd, w2_s, w2_scales)
         nc.sync.dma_start(list2[:], offs2)
-        load_scales(nc.scalar, nc.sync, xo_s[:], xo_scales)
+        load_low(nc.sync, xo_s, xo_scales)
+        load_low(nc.sync, w2_s, w2_scales)
         nc.sync.dma_start(out=w2_w[:].bitcast(I32), in_=words4(w2_words))
-        load_scales(nc.scalar, nc.sync, w2_s[:], w2_scales)
-        nc.sync.dma_start(out=xt_w[:].bitcast(I32), in_=words4(xt_words))
         nc.sync.dma_start(list1[:], offs)
-        load_scales(nc.scalar, nc.sync, xt_s[:], xt_scales)
-        nc.sync.dma_start(out=w_w[:].bitcast(I32), in_=w_words[0].bitcast(I32))
-        load_scales(nc.sync, nc.sync, w_s[:], w_scales)
-        nc.sync.dma_start(list3[:], offs3)
+        nc.sync.dma_start(out=xt_w[:].bitcast(I32), in_=words4(xt_words))
+        load_high(nc.gpsimd, xt_s, xt_scales)
+        load_high(nc.gpsimd, w_s, w_scales)
         nc.sync.dma_start(list4[:], offs4)
+        load_low(nc.sync, xt_s, xt_scales)
+        nc.sync.dma_start(out=w_w[:].bitcast(I32), in_=w_words[0].bitcast(I32))
+        load_low(nc.sync, w_s, w_scales)
+        nc.sync.dma_start(list3[:], offs3)
         nc.sync.dma_start(out=ws_w[:].bitcast(I32), in_=words4(ws_words))
+        load_low(nc.sync, ws_s, ws_scales)
         nc.sync.dma_start(out=wb_w[:].bitcast(I32), in_=words4(wb_words))
-        load_scales(nc.gpsimd, nc.gpsimd, ws_s[:], ws_scales)
-        load_scales(nc.gpsimd, nc.gpsimd, wb_s[:], wb_scales)
+        load_high(nc.sync, ws_s, ws_scales)
+        load_low(nc.sync, wb_s, wb_scales)
+        load_high(nc.sync, wb_s, wb_scales)
 
         def gather(name, table, offsets, dtype):
             picked = tile(name, J, dtype)
             nc.vector.tensor_copy(picked[:], table[:].indirect(offsets[:]))
             return picked
 
-        def deal(copy, name, src, dtype):
+        def deal(copy, name, src, dtype, walk):
             dealt = tile(name, R, dtype)
-            copy(dealt[:].rearrange("p (t m) -> p t m", t=PACK), src[:].rearrange("p (m t) -> p t m", t=PACK))
+            copy(dealt[:].rearrange("p (t m) -> " + walk, t=PACK), src.rearrange("p (m t) -> " + walk, t=PACK))
             return dealt
 
         xo_gw = gather("xo_gw", xo_w, list2, U16)
         xo_gs = gather("xo_gs", xo_s, list2, U8)
-        w2_dw = deal(nc.scalar.copy, "w2_dw", w2_w, U32)
-        w2_ds = deal(nc.vector.tensor_copy, "w2_ds", w2_s, U8)
-        w_dw = deal(nc.scalar.copy, "w_dw", w_w, U16)
+        w2_dw = deal(nc.scalar.copy, "w2_dw", w2_w[:], U32, "p m t")
+        w2_ds = deal(nc.vector.tensor_copy, "w2_ds", w2_s[:], U8, "p t m")
+        w_dw = deal(nc.scalar.copy, "w_dw", w_w[:], U16, "p m t")
         xt_gw = gather("xt_gw", xt_w, list1, U32)
+        xs_gw = gather("xs_gw", xt_w, list4, U32)
         xt_gs = gather("xt_gs", xt_s, list1, U8)
-        w_ds = deal(nc.vector.tensor_copy, "w_ds", w_s, U8)
+        w_ds = deal(nc.vector.tensor_copy, "w_ds", w_s[:], U8, "p t m")
+        xs_gs = gather("xs_gs", xt_s, list4, U8)
 
         b_sb = []
         for t in range(PACK):
             cols = slice(t * P, (t + 1) * P)
-            b_ps = ps.tile([P, J], F32, name="b_ps%d" % t)
+            b_ps = ps.tile([P, J], F32, name="b_ps", tag="bank%d" % t)
             nc.tensor.matmul_mx(
                 out=b_ps[:], lhsT=w2_dw[:, cols].bitcast(E5M2), lhsT_scale=w2_ds[:, cols],
                 rhs=xo_gw[:].bitcast(E2M1), rhs_scale=xo_gs[:], start=True, stop=True,
@@ -111,7 +120,7 @@ def tile_list_partner_twotab_further_plain_kernel(
 
         halves = [slice(h * HALF, (h + 1) * HALF) for h in range(2)]
         a_ps = [ps.tile([P, PACK, HALF], F32, name="a_ps%d" % h) for h in range(2)]
-        y_ps = [ps.tile([P, N // P, HALF], F32, name="y_ps%d" % h) for h in range(2)]
+        y_ps = [[ps.tile([P, HALF], F32, name="y_ps", tag="bank%d" % (2 * h + m)) for m in range(2)] for h in range(2)]
         partner = [sb.tile([P, PACK, HALF], F32, name="partner%d" % h, align_bytes=64) for h in range(2)]
         hid = [sb.tile([P, HALF, PACK], BF16, name="hid%d" % h, align_bytes=64) for h in range(2)]
         for h in range(2):
@@ -132,8 +141,8 @@ def tile_list_partner_twotab_further_plain_kernel(
 
         def larger(h):
             nc.vector.tensor_tensor(
-                out=hid[h][:], in0=a_ps[h][:].rearrange("p t j -> p j t"),
-                in1=partner[h][:].rearrange("p t j -> p j t"), op=MAX,
+                out=hid[h][:].rearrange("p (c i) t -> p c t i", i=4), in0=a_ps[h][:].rearrange("p t (c i) -> p c t i", i=4),
+                in1=partner[h][:].rearrange("p t (c i) -> p c t i", i=4), op=MAX,
             )
 
         def finish(h):
@@ -143,22 +152,21 @@ def tile_list_partner_twotab_further_plain_kernel(
             for m in range(N // P):
                 cols = slice(m * P, (m + 1) * P)
                 nc.tensor.matmul_mx(
-                    out=y_ps[h][:, m, :], lhsT=wb_w[:, cols].bitcast(E5M2), lhsT_scale=wb_s[:, cols],
-                    rhs=hid_w[:].bitcast(E4M3), rhs_scale=hid_s[:], start=False, stop=(m == N // P - 1),
+                    out=y_ps[h][m][:], lhsT=wb_w[:, cols].bitcast(E5M2), lhsT_scale=wb_s[:, cols],
+                    rhs=hid_w[:].bitcast(E4M3), rhs_scale=hid_s[:], start=False, stop=True,
                 )
             y = sb.tile([P, N // P, HALF], F32, name="y%d" % h, align_bytes=64)
-            nc.scalar.copy(y[:], y_ps[h][:])
+            nc.scalar.copy(y[:, 0, :], y_ps[h][0][:])
+            (nc.scalar.copy if h == 0 else nc.vector.tensor_copy)(y[:, 1, :], y_ps[h][1][:])
             nc.sync.dma_start(out=out.rearrange("(m p) j -> p m j", p=P)[:, :, halves[h]], in_=y[:])
 
-        xs_gw = gather("xs_gw", xt_w, list4, U32)
         larger(0)
-        xs_gs = gather("xs_gs", xt_s, list4, U8)
         for h in range(2):
             for m in range(N // P):
                 cols = slice(m * P, (m + 1) * P)
                 nc.tensor.matmul_mx(
-                    out=y_ps[h][:, m, :], lhsT=ws_w[:, cols].bitcast(E5M2), lhsT_scale=ws_s[:, cols],
-                    rhs=xs_gw[:, halves[h]].bitcast(E4M3), rhs_scale=xs_gs[:, halves[h]], start=(m == 0), stop=False,
+                    out=y_ps[h][m][:], lhsT=ws_w[:, cols].bitcast(E5M2), lhsT_scale=ws_s[:, cols],
+                    rhs=xs_gw[:, halves[h]].bitcast(E4M3), rhs_scale=xs_gs[:, halves[h]], start=True, stop=False,
                 )
         finish(0)
         larger(1)

@@ -69,13 +69,13 @@ def tile_list_partner_twotab_further_plain_kernel(
         load_low(nc.sync, xo_s, xo_scales)
         load_low(nc.sync, w2_s, w2_scales)
         nc.sync.dma_start(out=w2_w[:].bitcast(I32), in_=words4(w2_words))
-        nc.sync.dma_start(list1[:], offs)
+        nc.sync.dma_start(out=w_w[:].bitcast(I32), in_=w_words[0].bitcast(I32))
         nc.sync.dma_start(out=xt_w[:].bitcast(I32), in_=words4(xt_words))
         load_high(nc.gpsimd, xt_s, xt_scales)
         load_high(nc.gpsimd, w_s, w_scales)
+        nc.sync.dma_start(list1[:], offs)
         nc.sync.dma_start(list4[:], offs4)
         load_low(nc.sync, xt_s, xt_scales)
-        nc.sync.dma_start(out=w_w[:].bitcast(I32), in_=w_words[0].bitcast(I32))
         load_low(nc.sync, w_s, w_scales)
         nc.sync.dma_start(list3[:], offs3)
         nc.sync.dma_start(out=ws_w[:].bitcast(I32), in_=words4(ws_words))
@@ -103,7 +103,7 @@ def tile_list_partner_twotab_further_plain_kernel(
         xt_gw = gather("xt_gw", xt_w, list1, U32)
         xs_gw = gather("xs_gw", xt_w, list4, U32)
         xt_gs = gather("xt_gs", xt_s, list1, U8)
-        w_ds = deal(nc.vector.tensor_copy, "w_ds", w_s[:], U8, "p t m")
+        w_ds = deal(nc.gpsimd.tensor_copy, "w_ds", w_s[:], U8, "p t m")
         xs_gs = gather("xs_gs", xt_s, list4, U8)
 
         b_sb = []
@@ -134,7 +134,7 @@ def tile_list_partner_twotab_further_plain_kernel(
         for h in range(2):
             for t in range(PACK):
                 picked = b_sb[t][:].indirect(list3[:, h * HALF // 16 : (h + 1) * HALF // 16])
-                if h == 0 and t < 2:
+                if h == 0 and t < 1:
                     nc.vector.tensor_copy(partner[h][:, t, :], picked)
                 else:
                     nc.scalar.activation(out=partner[h][:, t, :], in_=picked, func=COPY)

@@ -62,28 +62,28 @@ def tile_list_partner_twotab_further_plain_kernel(
         def words4(ap):
             return ap[0].rearrange("p c t -> p (c t)").bitcast(I32)
 
+        load_low(nc.scalar, xo_s, xo_scales)
         nc.sync.dma_start(out=xo_w[:].bitcast(I32), in_=xo_words[0].bitcast(I32))
-        load_high(nc.scalar, xo_s, xo_scales)
-        load_high(nc.gpsimd, w2_s, w2_scales)
         nc.sync.dma_start(list2[:], offs2)
-        load_low(nc.sync, xo_s, xo_scales)
+        load_high(nc.scalar, w2_s, w2_scales)
         load_low(nc.sync, w2_s, w2_scales)
         nc.sync.dma_start(out=w2_w[:].bitcast(I32), in_=words4(w2_words))
-        nc.sync.dma_start(out=w_w[:].bitcast(I32), in_=w_words[0].bitcast(I32))
+        load_high(nc.sync, xo_s, xo_scales)
         nc.sync.dma_start(out=xt_w[:].bitcast(I32), in_=words4(xt_words))
-        load_high(nc.gpsimd, xt_s, xt_scales)
         load_high(nc.gpsimd, w_s, w_scales)
+        load_high(nc.gpsimd, xt_s, xt_scales)
+        load_high(nc.gpsimd, ws_s, ws_scales)
         nc.sync.dma_start(list1[:], offs)
+        nc.sync.dma_start(out=w_w[:].bitcast(I32), in_=w_words[0].bitcast(I32))
         nc.sync.dma_start(list4[:], offs4)
         load_low(nc.sync, xt_s, xt_scales)
-        load_low(nc.sync, w_s, w_scales)
         nc.sync.dma_start(list3[:], offs3)
+        load_low(nc.sync, w_s, w_scales)
         nc.sync.dma_start(out=ws_w[:].bitcast(I32), in_=words4(ws_words))
-        load_low(nc.sync, ws_s, ws_scales)
         nc.sync.dma_start(out=wb_w[:].bitcast(I32), in_=words4(wb_words))
-        load_high(nc.sync, ws_s, ws_scales)
-        load_low(nc.sync, wb_s, wb_scales)
         load_high(nc.sync, wb_s, wb_scales)
+        load_low(nc.sync, ws_s, ws_scales)
+        load_low(nc.sync, wb_s, wb_scales)
 
         def gather(name, table, offsets, dtype):
             picked = tile(name, J, dtype)
@@ -96,15 +96,12 @@ def tile_list_partner_twotab_further_plain_kernel(
             return dealt
 
         xo_gw = gather("xo_gw", xo_w, list2, U16)
-        xo_gs = gather("xo_gs", xo_s, list2, U8)
         w2_dw = deal(nc.scalar.copy, "w2_dw", w2_w[:], U32, "p m t")
         w2_ds = deal(nc.vector.tensor_copy, "w2_ds", w2_s[:], U8, "p t m")
-        w_dw = deal(nc.scalar.copy, "w_dw", w_w[:], U16, "p m t")
-        xt_gw = gather("xt_gw", xt_w, list1, U32)
-        xs_gw = gather("xs_gw", xt_w, list4, U32)
-        xt_gs = gather("xt_gs", xt_s, list1, U8)
-        w_ds = deal(nc.gpsimd.tensor_copy, "w_ds", w_s[:], U8, "p t m")
-        xs_gs = gather("xs_gs", xt_s, list4, U8)
+        xo_gs = gather("xo_gs", xo_s, list2, U8)
+
+        def scalar_copy(dst, src):
+            nc.scalar.activation(out=dst, in_=src, func=COPY)
 
         b_sb = []
         for t in range(PACK):
@@ -115,8 +112,19 @@ def tile_list_partner_twotab_further_plain_kernel(
                 rhs=xo_gw[:].bitcast(E2M1), rhs_scale=xo_gs[:], start=True, stop=True,
             )
             b_t = tile("b%d" % t, J, F32)
-            nc.scalar.activation(out=b_t[:], in_=b_ps[:], func=COPY)
+            (nc.vector.tensor_copy if t < 0 else scalar_copy)(b_t[:], b_ps[:])
             b_sb.append(b_t)
+
+        xt_gw = gather("xt_gw", xt_w, list1, U32)
+        xs_gw = gather("xs_gw", xt_w, list4, U32)
+        xt_gs = gather("xt_gs", xt_s, list1, U8)
+        w_dw = tile("w_dw", R, U16)
+        nc.gpsimd.tensor_copy(
+            w_dw[:].bitcast(U8).rearrange("p (t m e) -> p t m e", t=PACK, e=2),
+            w_w[:].bitcast(U8).rearrange("p (m t e) -> p t m e", t=PACK, e=2),
+        )
+        w_ds = deal(nc.gpsimd.tensor_copy, "w_ds", w_s[:], U8, "p t m")
+        xs_gs = gather("xs_gs", xt_s, list4, U8)
 
         halves = [slice(h * HALF, (h + 1) * HALF) for h in range(2)]
         a_ps = [ps.tile([P, PACK, HALF], F32, name="a_ps%d" % h) for h in range(2)]

from contextlib import ExitStack

import concourse.mybir as mybir

K, F, T, Z, J, R, N = 512, 512, 1024, 1024, 256, 512, 256
FLOPS = 2 * J * (K * R + F * R + R * N + K * N)

F32 = mybir.dt.float32
BF16 = mybir.dt.bfloat16
I32 = mybir.dt.int32
U32 = mybir.dt.uint32
U16 = mybir.dt.uint16
U8 = mybir.dt.uint8
E4M3 = mybir.dt.float8_e4m3fn_x4
E5M2 = mybir.dt.float8_e5m2_x4
E2M1 = mybir.dt.float4_e2m1fn_x4
COPY = mybir.ActivationFunctionType.Copy
MAX = mybir.AluOpType.max

P = 128
PACK = 4
HALF = J // 2


def load_low(queue, plane, scales):
    queue.dma_start(out=plane[0:16, :].bitcast(I32), in_=scales[0].bitcast(I32))


def load_high(queue, plane, scales):
    queue.dma_start(out=plane[16:128, :].bitcast(I32), in_=scales[0, 2:16, :].bitcast(I32).partition_broadcast(8))


def tile_list_partner_twotab_further_plain_kernel(
    tc, xt_words, xt_scales, w_words, w_scales, xo_words, xo_scales, w2_words, w2_scales,
    wb_words, wb_scales, ws_words, ws_scales, offs, offs2, offs3, offs4, out,
):
    nc = tc.nc
    with ExitStack() as ctx:
        sb = ctx.enter_context(tc.tile_pool(name="sb", bufs=1))
        ps = ctx.enter_context(tc.psum_pool(name="ps", bufs=1))

        def tile(name, cols, dtype):
            return sb.tile([P, cols], dtype, name=name, align_bytes=64)

        list1 = tile("list1", J // 16, U16)
        list2 = tile("list2", J // 16, U16)
        list3 = tile("list3", J // 16, U16)
        list4 = tile("list4", J // 16, U16)
        xt_w = tile("xt_w", T, U32)
        xt_s = tile("xt_s", T, U8)
        xo_w = tile("xo_w", Z, U16)
        xo_s = tile("xo_s", Z, U8)
        w_w = tile("w_w", R, U16)
        w2_w = tile("w2_w", R, U32)
        wb_w = tile("wb_w", N, U32)
        ws_w = tile("ws_w", N, U32)
        w2_s = tile("w2_s", R, U8)
        w_s = tile("w_s", R, U8)
        ws_s = tile("ws_s", N, U8)
        wb_s = tile("wb_s", N, U8)

        def words4(ap):
            return ap[0].rearrange("p c t -> p (c t)").bitcast(I32)

        load_low(nc.scalar, xo_s, xo_scales)
        nc.sync.dma_start(out=xo_w[:].bitcast(I32), in_=xo_words[0].bitcast(I32))
        nc.sync.dma_start(list2[:], offs2)
        load_high(nc.scalar, w2_s, w2_scales)
        load_low(nc.sync, w2_s, w2_scales)
        nc.sync.dma_start(out=w2_w[:].bitcast(I32), in_=words4(w2_words))
        load_high(nc.sync, xo_s, xo_scales)
        nc.sync.dma_start(out=xt_w[:].bitcast(I32), in_=words4(xt_words))
        load_high(nc.gpsimd, w_s, w_scales)
        load_high(nc.gpsimd, xt_s, xt_scales)
        load_high(nc.gpsimd, ws_s, ws_scales)
        nc.sync.dma_start(list1[:], offs)
        nc.sync.dma_start(out=w_w[:].bitcast(I32), in_=w_words[0].bitcast(I32))
        nc.sync.dma_start(list4[:], offs4)
        load_low(nc.sync, xt_s, xt_scales)
        nc.sync.dma_start(list3[:], offs3)
        load_low(nc.sync, w_s, w_scales)
        nc.sync.dma_start(out=ws_w[:].bitcast(I32), in_=words4(ws_words))
        nc.sync.dma_start(out=wb_w[:].bitcast(I32), in_=words4(wb_words))
        load_high(nc.sync, wb_s, wb_scales)
        load_low(nc.sync, ws_s, ws_scales)
        load_low(nc.sync, wb_s, wb_scales)

        def gather(name, table, offsets, dtype):
            picked = tile(name, J, dtype)
            nc.vector.tensor_copy(picked[:], table[:].indirect(offsets[:]))
            return picked

        def deal(copy, name, src, dtype, walk):
            dealt = tile(name, R, dtype)
            copy(dealt[:].rearrange("p (t m) -> " + walk, t=PACK), src.rearrange("p (m t) -> " + walk, t=PACK))
            return dealt

        xo_gw = gather("xo_gw", xo_w, list2, U16)
        w2_dw = deal(nc.scalar.copy, "w2_dw", w2_w[:], U32, "p m t")
        w2_ds = deal(nc.vector.tensor_copy, "w2_ds", w2_s[:], U8, "p t m")
        xo_gs = gather("xo_gs", xo_s, list2, U8)

        def scalar_copy(dst, src):
            nc.scalar.activation(out=dst, in_=src, func=COPY)

        b_sb = []
        for t in range(PACK):
            cols = slice(t * P, (t + 1) * P)
            b_ps = ps.tile([P, J], F32, name="b_ps", tag="bank%d" % t)
            nc.tensor.matmul_mx(
                out=b_ps[:], lhsT=w2_dw[:, cols].bitcast(E5M2), lhsT_scale=w2_ds[:, cols],
                rhs=xo_gw[:].bitcast(E2M1), rhs_scale=xo_gs[:], start=True, stop=True,
            )
            b_t = tile("b%d" % t, J, F32)
            (nc.vector.tensor_copy if t < 0 else scalar_copy)(b_t[:], b_ps[:])
            b_sb.append(b_t)

        xt_gw = gather("xt_gw", xt_w, list1, U32)
        xs_gw = gather("xs_gw", xt_w, list4, U32)
        xt_gs = gather("xt_gs", xt_s, list1, U8)
        w_dw = tile("w_dw", R, U16)
        nc.gpsimd.tensor_copy(
            w_dw[:].bitcast(U8).rearrange("p (t m e) -> p t m e", t=PACK, e=2),
            w_w[:].bitcast(U8).rearrange("p (m t e) -> p t m e", t=PACK, e=2),
        )
        w_ds = deal(nc.gpsimd.tensor_copy, "w_ds", w_s[:], U8, "p t m")
        xs_gs = gather("xs_gs", xt_s, list4, U8)

        halves = [slice(h * HALF, (h + 1) * HALF) for h in range(2)]
        a_ps = [ps.tile([P, PACK, HALF], F32, name="a_ps%d" % h) for h in range(2)]
        y_ps = [[ps.tile([P, HALF], F32, name="y_ps", tag="bank%d" % (2 * h + m)) for m in range(2)] for h in range(2)]
        partner = [sb.tile([P, PACK, HALF], F32, name="partner%d" % h, align_bytes=64) for h in range(2)]
        hid = [sb.tile([P, HALF, PACK], BF16, name="hid%d" % h, align_bytes=64) for h in range(2)]
        for h in range(2):
            for t in range(PACK):
                cols = slice(t * P, (t + 1) * P)
                nc.tensor.matmul_mx(
                    out=a_ps[h][:, t, :], lhsT=w_dw[:, cols].bitcast(E2M1), lhsT_scale=w_ds[:, cols],
                    rhs=xt_gw[:, halves[h]].bitcast(E4M3), rhs_scale=xt_gs[:, halves[h]], start=True, stop=True,
                )

        for h in range(2):
            for t in range(PACK):
                picked = b_sb[t][:].indirect(list3[:, h * HALF // 16 : (h + 1) * HALF // 16])
                if h == 0 and t < 1:
                    nc.vector.tensor_copy(partner[h][:, t, :], picked)
                else:
                    nc.scalar.activation(out=partner[h][:, t, :], in_=picked, func=COPY)

        def larger(h):
            nc.vector.tensor_tensor(
                out=hid[h][:].rearrange("p (c i) t -> p c t i", i=4), in0=a_ps[h][:].rearrange("p t (c i) -> p c t i", i=4),
                in1=partner[h][:].rearrange("p t (c i) -> p c t i", i=4), op=MAX,
            )

        def finish(h):
            hid_w = tile("hid_w%d" % h, HALF, U32)
            hid_s = tile("hid_s%d" % h, HALF, U8)
            nc.vector.quantize_mx(out=hid_w[:].bitcast(E4M3), scales=hid_s[:], in_=hid[h][:].rearrange("p j t -> p (j t)"))
            for m in range(N // P):
                cols = slice(m * P, (m + 1) * P)
                nc.tensor.matmul_mx(
                    out=y_ps[h][m][:], lhsT=wb_w[:, cols].bitcast(E5M2), lhsT_scale=wb_s[:, cols],
                    rhs=hid_w[:].bitcast(E4M3), rhs_scale=hid_s[:], start=False, stop=True,
                )
            y = sb.tile([P, N // P, HALF], F32, name="y%d" % h, align_bytes=64)
            nc.scalar.copy(y[:, 0, :], y_ps[h][0][:])
            (nc.scalar.copy if h == 0 else nc.vector.tensor_copy)(y[:, 1, :], y_ps[h][1][:])
            nc.sync.dma_start(out=out.rearrange("(m p) j -> p m j", p=P)[:, :, halves[h]], in_=y[:])

        larger(0)
        for h in range(2):
            for m in range(N // P):
                cols = slice(m * P, (m + 1) * P)
                nc.tensor.matmul_mx(
                    out=y_ps[h][m][:], lhsT=ws_w[:, cols].bitcast(E5M2), lhsT_scale=ws_s[:, cols],
                    rhs=xs_gw[:, halves[h]].bitcast(E4M3), rhs_scale=xs_gs[:, halves[h]], start=True, stop=False,
                )
        finish(0)
        larger(1)
        finish(1)
